import numpy as np
import ml_dtypes


def mxq(x, axis, fmt="e4m3"):
    dtype, down = {"e4m3": (ml_dtypes.float8_e4m3fn, 7), "e5m2": (ml_dtypes.float8_e5m2, 14)}[fmt]
    v = np.moveaxis(np.asarray(x, np.float32).astype(ml_dtypes.bfloat16).astype(np.float64), axis, -1)
    blocks = v.reshape(v.shape[:-1] + (-1, 32))
    amax = np.abs(blocks).max(-1, keepdims=True)
    byte = np.maximum(np.where(amax > 0, np.frexp(amax)[1] - 1 + 127, 0) - down, 1)
    scale = np.exp2(byte - 127.0)
    codes = (blocks / scale).astype(np.float32).astype(dtype).astype(np.float64)
    return np.moveaxis((codes * scale).reshape(v.shape), -1, axis)


WIDE = False


def mx_kscale(k):
    if not WIDE:
        return np.ones(k)
    levels = np.array([10, -10, 5, -5, 0])
    if k % 512:
        return np.exp2(np.random.permutation(np.resize(levels, k // 32))).repeat(32)
    a = np.empty((k // 512, 16))
    for p in range(k // 512):
        a[p, :8] = np.random.permutation(np.resize(levels, 8))
        for g in range(8):
            far = levels[np.abs(levels - a[p, g]) >= 10]
            a[p, g + 8] = far[np.random.randint(len(far))]
    return np.exp2(a.ravel()).repeat(32)


def f64(x):
    return np.asarray(x).astype(np.float64)


def striped(idx):
    return np.tile(idx.reshape(-1, 16).T, (8, 1)).astype(np.uint16)


def unstriped(offs):
    return offs[:16].T.reshape(-1).astype(np.int64)


E2M1 = np.array([0.0, 0.5, 1.0, 1.5, 2.0, 3.0, 4.0, 6.0, -0.0, -0.5, -1.0, -1.5, -2.0, -3.0, -4.0, -6.0])


def pack_weight(w, fmt):
    k, n = w.shape
    w = f64(np.asarray(w, np.float32).astype(ml_dtypes.bfloat16)).reshape(k // 32, 32, n)
    amax = np.abs(w).max(1)
    if fmt == "e4m3":
        byte = np.frexp(amax)[1] - 1 + 127 - 7
    else:
        mant, ex = np.frexp(amax / 6.0)
        byte = np.where(mant > 0.5, ex, ex - 1) + 127
    byte = np.clip(np.where(amax > 0, byte, 1), 1, 254)
    scaled = (w * np.exp2(127.0 - byte)[:, None, :]).reshape(k, n).astype(np.float32)
    by_word = np.ascontiguousarray(scaled.reshape(k // 512, 128, 4, n).transpose(0, 1, 3, 2))
    if fmt == "e4m3":
        words = by_word.astype(ml_dtypes.float8_e4m3fn).view(np.uint8)
    else:
        c = by_word.astype(ml_dtypes.float4_e2m1fn).view(np.uint8) & 0xF
        words = (c[..., 0::2] | (c[..., 1::2] << 4)).reshape(k // 512, 128, 2 * n)
    return np.ascontiguousarray(words), np.ascontiguousarray(byte.astype(np.uint8).reshape(k // 512, 16, n))


def unpack_weight(words, scales, fmt):
    g, _, n = scales.shape
    words = np.ascontiguousarray(words).reshape(g, 128, n, -1)
    if fmt == "e4m3":
        vals = words.view(ml_dtypes.float8_e4m3fn).astype(np.float64)
    else:
        nib = np.empty((g, 128, n, 4), np.uint8)
        nib[..., 0::2] = words & 0xF
        nib[..., 1::2] = words >> 4
        vals = E2M1[nib]
    vals = vals * np.repeat(np.exp2(scales.astype(np.float64) - 127.0), 8, axis=1)[..., None]
    return vals.transpose(0, 1, 3, 2).reshape(g * 512, n)


def gelu(v):
    return 0.5 * v * (1.0 + np.tanh(np.sqrt(2.0 / np.pi) * (v + 0.044715 * v**3)))


K, T, S, P, H, N = 1024, 4096, 1024, 512, 1024, 512


def setup_inputs():
    n = np.random.standard_normal
    s = mx_kscale(K)[:, None]
    u = mx_kscale(H)[:, None]
    d = {}
    d["tab_words"], d["tab_scales"] = pack_weight(n((K, T)) * s, "e2m1")
    d["offs"] = striped(np.random.permutation(T)[:S])
    d["pos1"] = striped(np.random.permutation(S)[:P])
    d["pos2"] = striped(np.random.permutation(S)[:P])
    d["w1"] = (1.3 * n((K, H)) / K ** 0.5 / s).astype(np.float32)
    d["b1"] = (0.5 * n(H)).astype(np.float32)
    d["w2_words"], d["w2_scales"] = pack_weight(1.9 * n((K, H)) / K ** 0.5 / s, "e4m3")
    d["gz"] = (np.exp(0.3 * n(H)) * u[:, 0]).astype(np.float32)
    d["gt"] = (1.2 * np.exp(0.3 * n(H)) * u[:, 0]).astype(np.float32)
    d["w3_words"], d["w3_scales"] = pack_weight(n((H, N)) / H ** 0.5 / u, "e2m1")
    d["w4"] = (n((H, N)) / H ** 0.5 / u).astype(np.float32)
    return d


def reference(tab_words, tab_scales, offs, pos1, pos2, w1, b1, w2_words, w2_scales,
              gz, gt, w3_words, w3_scales, w4):
    v = unpack_weight(tab_words, tab_scales, "e2m1")[:, unstriped(offs)]
    w2 = unpack_weight(w2_words, w2_scales, "e4m3")
    w3 = unpack_weight(w3_words, w3_scales, "e2m1")
    h1 = (mxq(f64(w1), 0, "e4m3").T @ v) + f64(b1)[:, None]
    m2 = w2.T @ v
    h2 = m2 / (1.0 + np.exp(-m2))
    z = np.minimum(h1[:, unstriped(pos1)], h2[:, unstriped(pos2)]) * f64(gz)[:, None]
    x = np.tanh(h1[:, unstriped(pos2)]) * f64(gt)[:, None]
    zq = mxq(z, 0, "e4m3")
    xq = mxq(x, 0, "e4m3")
    return w3.T @ zq + mxq(f64(w4), 0, "e4m3").T @ xq

@@ -1,0 +1,310 @@
+from contextlib import ExitStack
+
+import concourse.mybir as mybir
+
+K, T, S, PAIRS, H, N = 1024, 4096, 1024, 512, 1024, 512
+FLOPS = 2 * 2 * K * H * S + 2 * 2 * H * N * PAIRS
+
+F32 = mybir.dt.float32
+BF16 = mybir.dt.bfloat16
+I32 = mybir.dt.int32
+U32 = mybir.dt.uint32
+U16 = mybir.dt.uint16
+U8 = mybir.dt.uint8
+FP8X4 = mybir.dt.float8_e4m3fn_x4
+FP4X4 = mybir.dt.float4_e2m1fn_x4
+ACT = mybir.ActivationFunctionType
+ALU = mybir.AluOpType
+
+P = 128
+PACK = 4
+KP = P * PACK
+BANK = 512
+
+
+def tile_list_sumo_bout_features_kernel(
+    tc, tab_words, tab_scales, offs, pos1, pos2, w1, b1, w2_words, w2_scales, gz, gt, w3_words, w3_scales, w4, out
+):
+    nc = tc.nc
+    with ExitStack() as ctx:
+        lists = ctx.enter_context(tc.tile_pool(name="lists", bufs=1))
+        keep = ctx.enter_context(tc.tile_pool(name="keep", bufs=1))
+        ring = ctx.enter_context(tc.tile_pool(name="ring", bufs=2))
+        ps1 = ctx.enter_context(tc.psum_pool(name="ps1", bufs=4))
+        ps2 = ctx.enter_context(tc.psum_pool(name="ps2", bufs=1))
+
+        offs_t = lists.tile([P, S // 16], U16, name="offs_t")
+        nc.sync.dma_start(offs_t[:], offs)
+        tsc = ring.tile([P, T], U8, name="tsc", tag="rawA", bufs=1, align_bytes=64)
+        nc.sync.dma_start(tsc[0:32, :].bitcast(I32), tab_scales.rearrange("a q t -> q a t").bitcast(I32))
+        nc.vector.memset(tsc[32:64, :].bitcast(I32), 0)
+        nc.vector.memset(tsc[64:P, :].bitcast(I32), 0)
+        pos2_t = lists.tile([P, PAIRS // 16], U16, name="pos2_t")
+        nc.sync.dma_start(pos2_t[:], pos2)
+        pos1_t = lists.tile([P, PAIRS // 16], U16, name="pos1_t")
+        nc.sync.dma_start(pos1_t[:], pos1)
+        tw = []
+        for a in range(2):
+            t_a = ring.tile([P, T], U16, name="tw%d" % a, tag=("rawB", "w2c0")[a], bufs=1, align_bytes=64)
+            nc.sync.dma_start(t_a[:].bitcast(I32), tab_words[a].bitcast(I32))
+            tw.append(t_a)
+
+        w2s_raw = ring.tile([P, 2, H], U8, name="w2s_raw", tag="wsc", bufs=1, align_bytes=64)
+        nc.gpsimd.memset(w2s_raw[:].bitcast(I32), 0)
+        for q in range(4):
+            nc.gpsimd.dma_start(
+                w2s_raw[32 * q : 32 * q + 4, :, :].bitcast(I32),
+                w2_scales[:, 4 * q : 4 * q + 4, :].rearrange("a r c -> r a c").bitcast(I32),
+            )
+        tplane = keep.tile([P, 2, S], U8, name="tplane", align_bytes=64)
+        nc.vector.memset(tplane[:].bitcast(I32), 0)
+        warm = keep.tile([P, 8], F32, name="warm")
+        nc.vector.memset(warm[:, 0:4], 0.0)
+        nc.scalar.activation(warm[:, 4:8], warm[:, 0:4], ACT.Silu)
+        vecs = []
+        for name, vec in (("b1t", b1), ("gzt", gz), ("gtt", gt)):
+            v_t = keep.tile([P, 2, PACK], F32, name=name)
+            nc.gpsimd.dma_start(v_t[:], vec.rearrange("(b p t) -> p b t", b=2, t=PACK))
+            vecs.append(v_t)
+        b1t, gzt, gtt = vecs
+
+        w2_all = w2_words.rearrange("a p c i -> p a (c i)").bitcast(I32)
+        w2_raw = {}
+        w1_raw = {}
+        w4_raw = {}
+
+        def load_w2(b, tag, bufs):
+            w_b = ring.tile([P, 2, KP], I32, name="w2raw%d" % b, tag=tag, bufs=bufs, align_bytes=64)
+            nc.sync.dma_start(w_b[:], w2_all[:, :, KP * b : KP * (b + 1)])
+            w2_raw[b] = w_b
+
+        def load_w1(a, b, tag, bufs):
+            raw = ring.tile([P, PACK, KP], F32, name="w1raw%d%d" % (a, b), tag=tag, bufs=bufs, align_bytes=64)
+            nc.sync.dma_start(
+                raw[:], w1[KP * a : KP * (a + 1), KP * b : KP * (b + 1)].rearrange("(p j) c -> p j c", j=PACK)
+            )
+            w1_raw[(a, b)] = raw
+
+        def load_w4(b, tag, bufs):
+            raw = ring.tile([P, PACK, N], F32, name="w4raw%d" % b, tag=tag, bufs=bufs, align_bytes=64)
+            nc.sync.dma_start(raw[:], w4[KP * b : KP * (b + 1), :].rearrange("(p j) n -> p j n", j=PACK))
+            w4_raw[b] = raw
+
+        load_w2(0, "rawC", 1)
+
+        gsc = keep.tile([P, S], U8, name="gsc", align_bytes=64)
+        nc.vector.tensor_copy(gsc[:], tsc[:].indirect(offs_t[:]))
+        for q in range(4):
+            nc.scalar.dma_start(tplane[32 * q : 32 * q + 4, :, :].bitcast(I32), gsc[8 * q : 8 * q + 8, :].bitcast(I32))
+        planes = [tplane[:, 0, :], tplane[:, 1, :]]
+        load_w1(0, 0, "rawA", 1)
+        gw = []
+        for a in range(2):
+            g_a = keep.tile([P, S], U16, name="gw%d" % a, align_bytes=64)
+            nc.vector.tensor_copy(g_a[:], tw[a][:].indirect(offs_t[:]))
+            gw.append(g_a)
+        load_w1(1, 0, "rawB", 1)
+
+        w3 = {}
+
+        def load_w3():
+            w3["w"] = ring.tile([P, 2, 2 * N], U8, name="w3w", tag="rawC", bufs=1, align_bytes=64)
+            nc.sync.dma_start(w3["w"][:].bitcast(I32), w3_words.rearrange("a p c -> p a c").bitcast(I32))
+
+        def load_w3_scales():
+            w3["s"] = ring.tile([P, 2, N], U8, name="w3s", tag="wsc", bufs=1, align_bytes=64)
+            nc.gpsimd.memset(w3["s"][:].bitcast(I32), 0)
+            for q in range(4):
+                nc.sync.dma_start(
+                    w3["s"][32 * q : 32 * q + 4, :, :].bitcast(I32),
+                    w3_scales[:, 4 * q : 4 * q + 4, :].rearrange("a r c -> r a c").bitcast(I32),
+                )
+
+        w2c, w2s = {}, {}
+
+        def deal_w2(b):
+            codes = ring.tile([P, 2, KP], I32, name="w2c%d" % b, bufs=1, align_bytes=64)
+            nc.vector.tensor_copy(
+                codes[:].rearrange("p a (t c i) -> p a c t i", t=4, i=4),
+                w2_raw[b][:].rearrange("p a (c i t) -> p a c t i", t=4, i=4),
+            )
+            scales = keep.tile([P, 2, KP], U8, name="w2s%d" % b, align_bytes=64)
+            nc.vector.tensor_copy(
+                scales[:].rearrange("p a (t c i) -> p a c t i", t=4, i=16),
+                w2s_raw[:, :, KP * b : KP * (b + 1)].rearrange("p a (c i t) -> p a c t i", t=4, i=16),
+            )
+            for a in range(2):
+                w2c[(a, b)] = codes[:, a, :]
+                w2s[(a, b)] = scales[:, a, :]
+
+        w1c, w1s = {}, {}
+
+        def quantise(grouped, name):
+            codes = keep.tile([P, KP], U32, name=name + "c", align_bytes=64)
+            scales = keep.tile([P, KP], U8, name=name + "s", align_bytes=64)
+            nc.vector.quantize_mx(out=codes[:].bitcast(FP8X4), scales=scales[:], in_=grouped[:])
+            return codes[:], scales[:]
+
+        def prep_w1(a, b, on_vector):
+            grouped = ring.tile([P, KP * PACK], BF16, name="wg", tag="grouped", align_bytes=64)
+            dst = grouped[:].rearrange("p (t m j) -> p m t j", t=4, j=4)
+            src = w1_raw[(a, b)][:].rearrange("p j (m t) -> p m t j", t=4)
+            if on_vector:
+                nc.vector.tensor_copy(dst, src)
+            else:
+                nc.scalar.copy(dst, src)
+            w1c[(a, b)], w1s[(a, b)] = quantise(grouped, "w1q%d%d" % (a, b))
+
+        w4c, w4s = {}, {}
+
+        def prep_w4(b):
+            grouped = ring.tile([P, N * PACK], BF16, name="wg", tag="grouped", align_bytes=64)
+            nc.scalar.copy(
+                grouped[:].rearrange("p (c i j) -> p c j i", i=4, j=4),
+                w4_raw[b][:].rearrange("p j (c i) -> p c j i", i=4),
+            )
+            w4c[b], w4s[b] = quantise(grouped, "w4q%d" % b)
+
+        def first_stage(codes, scales, b, t, window, func, bias):
+            cols = slice(P * t, P * (t + 1))
+            for half in range(2):
+                picked = slice(BANK * half, BANK * (half + 1))
+                bank = ps1.tile([P, BANK], F32, name="bank")
+                for a in range(2):
+                    nc.tensor.matmul_mx(
+                        out=bank[:],
+                        lhsT=codes[(a, b)][:, cols].bitcast(FP8X4),
+                        lhsT_scale=scales[(a, b)][:, cols],
+                        rhs=gw[a][:, picked].bitcast(FP4X4),
+                        rhs_scale=planes[a][:, picked],
+                        start=(a == 0),
+                        stop=(a == 1),
+                    )
+                nc.scalar.activation(window[:, picked], bank[:], func, bias=bias)
+
+        h1, h2, grip1, grip2, least, rows = {}, {}, {}, {}, {}, {}
+
+        def make_h2(s):
+            h2[s] = ring.tile([P, S], F32, name="h2", bufs=4)
+            first_stage(w2c, w2s, s // 4, s % 4, h2[s], ACT.Silu, 0.0)
+
+        def pick_h2(s):
+            grip2[s] = ring.tile([P, PAIRS], F32, name="grip2", bufs=6)
+            nc.vector.tensor_copy(grip2[s][:], h2[s][:].indirect(pos2_t[:]))
+
+        def make_h1(s):
+            h1[s] = ring.tile([P, S], F32, name="h1", bufs=5)
+            first_stage(w1c, w1s, s // 4, s % 4, h1[s], ACT.Identity, b1t[:, s // 4, s % 4 : s % 4 + 1])
+
+        def pick_h1(s):
+            grip1[s] = ring.tile([P, PAIRS], F32, name="grip1", bufs=4)
+            nc.vector.tensor_copy(grip1[s][:], h1[s][:].indirect(pos2_t[:]))
+            charge = ring.tile([P, PAIRS], F32, name="charge", bufs=2)
+            nc.vector.tensor_copy(charge[:], h1[s][:].indirect(pos1_t[:]))
+            least[s] = ring.tile([P, PAIRS], F32, name="least", bufs=4)
+            nc.vector.tensor_tensor(least[s][:], charge[:], grip2[s][:], ALU.min)
+
+        def features(s, z_on_vector=False):
+            b, t = s // 4, s % 4
+            if t == 0:
+                rows[("z", b)] = ring.tile([P, PACK, PAIRS], BF16, name="zrows")
+                rows[("x", b)] = ring.tile([P, PACK, PAIRS], BF16, name="xrows")
+            bounded = ring.tile([P, PAIRS], F32, name="bounded", bufs=2)
+            nc.scalar.activation(bounded[:], grip1[s][:], ACT.Tanh)
+            nc.scalar.activation(rows[("x", b)][:, t, :], bounded[:], ACT.Copy, scale=gtt[:, b, t : t + 1])
+            if z_on_vector:
+                nc.vector.tensor_scalar(rows[("z", b)][:, t, :], least[s][:], gzt[:, b, t : t + 1], None, ALU.mult)
+            else:
+                nc.scalar.activation(rows[("z", b)][:, t, :], least[s][:], ACT.Copy, scale=gzt[:, b, t : t + 1])
+
+        acc = [ps2.tile([P, PAIRS], F32, name="acc%d" % j) for j in range(4)]
+
+        def second_stage(kind, b, first, last, on_vector):
+            grouped = ring.tile([P, PAIRS * PACK], BF16, name="fg", tag="fgrouped%d" % b, bufs=2 - b, align_bytes=64)
+            dst = grouped[:].rearrange("p (c i t) -> p c t i", i=4, t=4)
+            src = rows[(kind, b)][:].rearrange("p t (c i) -> p c t i", i=4)
+            if on_vector:
+                nc.vector.tensor_copy(dst, src)
+            else:
+                nc.scalar.copy(dst, src)
+            codes, scales = quantise(grouped, "%sq%d" % (kind, b))
+            for j in range(4):
+                cols = slice(P * j, P * (j + 1))
+                if kind == "z":
+                    lhs = w3["w"][:, b, 2 * P * j : 2 * P * (j + 1)].bitcast(FP4X4)
+                    lhs_scale = w3["s"][:, b, cols]
+                else:
+                    lhs = w4c[b][:, cols].bitcast(FP8X4)
+                    lhs_scale = w4s[b][:, cols]
+                nc.tensor.matmul_mx(
+                    out=acc[j][:], lhsT=lhs, lhsT_scale=lhs_scale, rhs=codes.bitcast(FP8X4), rhs_scale=scales,
+                    start=first, stop=last,
+                )
+
+        deal_w2(0)
+        load_w3()
+        prep_w1(0, 0, False)
+        load_w2(1, "rawA", 1)
+        make_h2(0)
+        prep_w1(1, 0, True)
+        load_w1(0, 1, "rawB", 1)
+        make_h2(1)
+        pick_h2(0)
+        make_h2(2)
+        make_h1(0)
+        make_h2(3)
+        pick_h2(1)
+        deal_w2(1)
+        load_w1(1, 1, "rawA", 1)
+        load_w3_scales()
+        make_h1(1)
+        pick_h2(2)
+        pick_h1(0)
+        make_h1(2)
+        make_h1(3)
+        pick_h2(3)
+        prep_w1(0, 1, False)
+        load_w4(0, "rawB", 1)
+        prep_w1(1, 1, False)
+        load_w4(1, "rawA", 1)
+        pick_h1(1)
+        make_h2(4)
+        features(0)
+        make_h2(5)
+        pick_h1(2)
+        features(1)
+        make_h2(6)
+        make_h2(7)
+        pick_h1(3)
+        make_h1(4)
+        features(2)
+        pick_h2(4)
+        pick_h2(5)
+        make_h1(5)
+        features(3)
+        pick_h2(6)
+        pick_h2(7)
+        make_h1(6)
+        pick_h1(4)
+        make_h1(7)
+        prep_w4(0)
+        pick_h1(5)
+        second_stage("z", 0, True, False, False)
+        features(4)
+        prep_w4(1)
+        pick_h1(6)
+        second_stage("x", 0, False, False, True)
+        features(5)
+        pick_h1(7)
+        features(6, True)
+        features(7, True)
+        second_stage("z", 1, False, False, True)
+        second_stage("x", 1, False, True, True)
+
+        for j in range(4):
+            res = ring.tile([P, PAIRS], F32, name="res", tag="grip2", bufs=6)
+            if j % 2 == 0:
+                nc.scalar.copy(res[:], acc[j][:])
+            else:
+                nc.vector.tensor_copy(res[:], acc[j][:])
+            nc.sync.dma_start(out[P * j : P * (j + 1), :], res[:])

@@ -30,112 +30,115 @@ def tile_list_sumo_bout_features_kernel(
         lists = ctx.enter_context(tc.tile_pool(name="lists", bufs=1))
         keep = ctx.enter_context(tc.tile_pool(name="keep", bufs=1))
         ring = ctx.enter_context(tc.tile_pool(name="ring", bufs=2))
-        ps1 = ctx.enter_context(tc.psum_pool(name="ps1", bufs=4))
-        ps2 = ctx.enter_context(tc.psum_pool(name="ps2", bufs=1))
+        psum = ctx.enter_context(tc.psum_pool(name="psum", bufs=8))
+
+        w2_all = w2_words.rearrange("a p c i -> p a (c i)").bitcast(I32)
+        w2_raw, w1_raw, w4_raw, w3, w2c, w2s = {}, {}, {}, {}, {}, {}
+
+        def once(shape, dtype, name, slot):
+            return ring.tile(shape, dtype, name=name, tag=slot, bufs=1, align_bytes=64)
+
+        def load_table(a, slot):
+            words = once([P, T], U16, "tw%d" % a, slot)
+            nc.sync.dma_start(words[:].bitcast(I32), tab_words[a].bitcast(I32))
+            return words
+
+        def load_w2(b, slot):
+            w2_raw[b] = once([P, 2, KP], I32, "w2raw%d" % b, slot)
+            nc.sync.dma_start(w2_raw[b][:], w2_all[:, :, KP * b : KP * (b + 1)])
+
+        def load_w1(a, b, slot):
+            w1_raw[(a, b)] = once([P, PACK, KP], F32, "w1raw%d%d" % (a, b), slot)
+            nc.sync.dma_start(
+                w1_raw[(a, b)][:],
+                w1[KP * a : KP * (a + 1), KP * b : KP * (b + 1)].rearrange("(p j) c -> p j c", j=PACK),
+            )
+
+        def load_w4(b, slot):
+            w4_raw[b] = once([P, PACK, N], F32, "w4raw%d" % b, slot)
+            nc.sync.dma_start(w4_raw[b][:], w4[KP * b : KP * (b + 1), :].rearrange("(p j) n -> p j n", j=PACK))
+
+        def load_scale_rows(queue, scales, width, name, slot):
+            plane = once([P, 2, width], U8, name, slot)
+            nc.gpsimd.memset(plane[:].bitcast(I32), 0)
+            for q in range(4):
+                queue.dma_start(
+                    plane[32 * q : 32 * q + 4, :, :].bitcast(I32),
+                    scales[:, 4 * q : 4 * q + 4, :].rearrange("a r c -> r a c").bitcast(I32),
+                )
+            return plane
 
         offs_t = lists.tile([P, S // 16], U16, name="offs_t")
         nc.sync.dma_start(offs_t[:], offs)
-        tsc = ring.tile([P, T], U8, name="tsc", tag="rawA", bufs=1, align_bytes=64)
+        w2s_raw = once([P, H], U8, "w2s_raw", "F")
+        nc.sync.dma_start(w2s_raw[0:32, :].bitcast(I32), w2_scales.rearrange("a q c -> q a c").bitcast(I32))
+        tsc = once([P, T], U8, "tsc", "A")
         nc.sync.dma_start(tsc[0:32, :].bitcast(I32), tab_scales.rearrange("a q t -> q a t").bitcast(I32))
-        nc.vector.memset(tsc[32:64, :].bitcast(I32), 0)
-        nc.vector.memset(tsc[64:P, :].bitcast(I32), 0)
+        for rows_tile in (w2s_raw, tsc):
+            nc.vector.memset(rows_tile[32:64, :].bitcast(I32), 0)
+            nc.vector.memset(rows_tile[64:P, :].bitcast(I32), 0)
         pos2_t = lists.tile([P, PAIRS // 16], U16, name="pos2_t")
         nc.sync.dma_start(pos2_t[:], pos2)
         pos1_t = lists.tile([P, PAIRS // 16], U16, name="pos1_t")
         nc.sync.dma_start(pos1_t[:], pos1)
-        tw = []
-        for a in range(2):
-            t_a = ring.tile([P, T], U16, name="tw%d" % a, tag=("rawB", "w2c0")[a], bufs=1, align_bytes=64)
-            nc.sync.dma_start(t_a[:].bitcast(I32), tab_words[a].bitcast(I32))
-            tw.append(t_a)
-
-        w2s_raw = ring.tile([P, 2, H], U8, name="w2s_raw", tag="wsc", bufs=1, align_bytes=64)
-        nc.gpsimd.memset(w2s_raw[:].bitcast(I32), 0)
-        for q in range(4):
-            nc.gpsimd.dma_start(
-                w2s_raw[32 * q : 32 * q + 4, :, :].bitcast(I32),
-                w2_scales[:, 4 * q : 4 * q + 4, :].rearrange("a r c -> r a c").bitcast(I32),
-            )
+        b1t = keep.tile([P, 2, PACK], F32, name="b1t")
+        nc.sync.dma_start(b1t[:], b1.rearrange("(b p t) -> p b t", b=2, t=PACK))
+        tw0 = load_table(0, "C")
+        load_w1(0, 0, "B")
+        load_w2(0, "E")
+        tw1 = load_table(1, "G")
+        warm = keep.tile([P, 8], F32, name="warm")
+        nc.gpsimd.memset(warm[:, 0:4], 0.0)
+        nc.scalar.activation(warm[:, 4:8], warm[:, 0:4], ACT.Silu)
+        w2plane = keep.tile([P, 2, H], U8, name="w2plane", align_bytes=64)
+        nc.gpsimd.memset(w2plane[:].bitcast(I32), 0)
         tplane = keep.tile([P, 2, S], U8, name="tplane", align_bytes=64)
         nc.vector.memset(tplane[:].bitcast(I32), 0)
-        warm = keep.tile([P, 8], F32, name="warm")
-        nc.vector.memset(warm[:, 0:4], 0.0)
-        nc.scalar.activation(warm[:, 4:8], warm[:, 0:4], ACT.Silu)
-        vecs = []
-        for name, vec in (("b1t", b1), ("gzt", gz), ("gtt", gt)):
-            v_t = keep.tile([P, 2, PACK], F32, name=name)
-            nc.gpsimd.dma_start(v_t[:], vec.rearrange("(b p t) -> p b t", b=2, t=PACK))
-            vecs.append(v_t)
-        b1t, gzt, gtt = vecs
 
-        w2_all = w2_words.rearrange("a p c i -> p a (c i)").bitcast(I32)
-        w2_raw = {}
-        w1_raw = {}
-        w4_raw = {}
-
-        def load_w2(b, tag, bufs):
-            w_b = ring.tile([P, 2, KP], I32, name="w2raw%d" % b, tag=tag, bufs=bufs, align_bytes=64)
-            nc.sync.dma_start(w_b[:], w2_all[:, :, KP * b : KP * (b + 1)])
-            w2_raw[b] = w_b
-
-        def load_w1(a, b, tag, bufs):
-            raw = ring.tile([P, PACK, KP], F32, name="w1raw%d%d" % (a, b), tag=tag, bufs=bufs, align_bytes=64)
-            nc.sync.dma_start(
-                raw[:], w1[KP * a : KP * (a + 1), KP * b : KP * (b + 1)].rearrange("(p j) c -> p j c", j=PACK)
-            )
-            w1_raw[(a, b)] = raw
-
-        def load_w4(b, tag, bufs):
-            raw = ring.tile([P, PACK, N], F32, name="w4raw%d" % b, tag=tag, bufs=bufs, align_bytes=64)
-            nc.sync.dma_start(raw[:], w4[KP * b : KP * (b + 1), :].rearrange("(p j) n -> p j n", j=PACK))
-            w4_raw[b] = raw
-
-        load_w2(0, "rawC", 1)
-
-        gsc = keep.tile([P, S], U8, name="gsc", align_bytes=64)
-        nc.vector.tensor_copy(gsc[:], tsc[:].indirect(offs_t[:]))
-        for q in range(4):
-            nc.scalar.dma_start(tplane[32 * q : 32 * q + 4, :, :].bitcast(I32), gsc[8 * q : 8 * q + 8, :].bitcast(I32))
-        planes = [tplane[:, 0, :], tplane[:, 1, :]]
-        load_w1(0, 0, "rawA", 1)
-        gw = []
-        for a in range(2):
-            g_a = keep.tile([P, S], U16, name="gw%d" % a, align_bytes=64)
-            nc.vector.tensor_copy(g_a[:], tw[a][:].indirect(offs_t[:]))
-            gw.append(g_a)
-        load_w1(1, 0, "rawB", 1)
-
-        w3 = {}
-
-        def load_w3():
-            w3["w"] = ring.tile([P, 2, 2 * N], U8, name="w3w", tag="rawC", bufs=1, align_bytes=64)
-            nc.sync.dma_start(w3["w"][:].bitcast(I32), w3_words.rearrange("a p c -> p a c").bitcast(I32))
-
-        def load_w3_scales():
-            w3["s"] = ring.tile([P, 2, N], U8, name="w3s", tag="wsc", bufs=1, align_bytes=64)
-            nc.gpsimd.memset(w3["s"][:].bitcast(I32), 0)
-            for q in range(4):
-                nc.sync.dma_start(
-                    w3["s"][32 * q : 32 * q + 4, :, :].bitcast(I32),
-                    w3_scales[:, 4 * q : 4 * q + 4, :].rearrange("a r c -> r a c").bitcast(I32),
+        def spread_rows(queues, plane, rows_tile):
+            for q, queue in enumerate(queues):
+                queue.dma_start(
+                    plane[32 * q : 32 * q + 4, :, :].bitcast(I32), rows_tile[8 * q : 8 * q + 8, :].bitcast(I32)
                 )
 
-        w2c, w2s = {}, {}
+        w2s_dealt = once([P, H], U8, "w2s_dealt", "H")
+        nc.vector.tensor_copy(
+            w2s_dealt[:].rearrange("p (b t c i) -> p b c t i", b=2, t=4, i=16),
+            w2s_raw[:].rearrange("p (b c i t) -> p b c t i", b=2, t=4, i=16),
+        )
+        spread_rows((nc.gpsimd,) * 4, w2plane, w2s_dealt)
+        gains = once([P, 2, 2, PACK], F32, "gains", "H")
+        for i, vec in enumerate((gz, gt)):
+            nc.gpsimd.dma_start(gains[:, i, :, :], vec.rearrange("(b p t) -> p b t", b=2, t=PACK))
+        gzt, gtt = gains[:, 0, :, :], gains[:, 1, :, :]
+
+        gsc = once([P, S], U8, "gsc", "D")
+        nc.vector.tensor_copy(gsc[:], tsc[:].indirect(offs_t[:]))
+        spread_rows((nc.scalar,) * 4, tplane, gsc)
+        planes = [tplane[:, 0, :], tplane[:, 1, :]]
+        gw = [keep.tile([P, S], U16, name="gw%d" % a, align_bytes=64) for a in range(2)]
+        nc.vector.tensor_copy(gw[0][:], tw0[:].indirect(offs_t[:]))
+        load_w1(1, 0, "C")
+
+        def gather_second_pass():
+            for half in range(2):
+                nc.vector.tensor_copy(
+                    gw[1][:, BANK * half : BANK * (half + 1)], tw1[:].indirect(offs_t[:, 32 * half : 32 * (half + 1)])
+                )
+
+        def load_w3():
+            w3["w"] = once([P, 2, 2 * N], U8, "w3w", "G")
+            nc.sync.dma_start(w3["w"][:].bitcast(I32), w3_words.rearrange("a p c -> p a c").bitcast(I32))
 
         def deal_w2(b):
-            codes = ring.tile([P, 2, KP], I32, name="w2c%d" % b, bufs=1, align_bytes=64)
+            codes = keep.tile([P, 2, KP], I32, name="w2c%d" % b, align_bytes=64)
             nc.vector.tensor_copy(
                 codes[:].rearrange("p a (t c i) -> p a c t i", t=4, i=4),
                 w2_raw[b][:].rearrange("p a (c i t) -> p a c t i", t=4, i=4),
             )
-            scales = keep.tile([P, 2, KP], U8, name="w2s%d" % b, align_bytes=64)
-            nc.vector.tensor_copy(
-                scales[:].rearrange("p a (t c i) -> p a c t i", t=4, i=16),
-                w2s_raw[:, :, KP * b : KP * (b + 1)].rearrange("p a (c i t) -> p a c t i", t=4, i=16),
-            )
             for a in range(2):
                 w2c[(a, b)] = codes[:, a, :]
-                w2s[(a, b)] = scales[:, a, :]
+                w2s[(a, b)] = w2plane[:, a, KP * b : KP * (b + 1)]
 
         w1c, w1s = {}, {}
 
@@ -146,7 +149,7 @@ def tile_list_sumo_bout_features_kernel(
             return codes[:], scales[:]
 
         def prep_w1(a, b, on_vector):
-            grouped = ring.tile([P, KP * PACK], BF16, name="wg", tag="grouped", align_bytes=64)
+            grouped = once([P, KP * PACK], BF16, "wg", (("first", "I"), ("after_w1_0", "after_w1_1"))[b][a])
             dst = grouped[:].rearrange("p (t m j) -> p m t j", t=4, j=4)
             src = w1_raw[(a, b)][:].rearrange("p j (m t) -> p m t j", t=4)
             if on_vector:
@@ -158,7 +161,7 @@ def tile_list_sumo_bout_features_kernel(
         w4c, w4s = {}, {}
 
         def prep_w4(b):
-            grouped = ring.tile([P, N * PACK], BF16, name="wg", tag="grouped", align_bytes=64)
+            grouped = once([P, N * PACK], BF16, "wg", "after_w4_%d" % b)
             nc.scalar.copy(
                 grouped[:].rearrange("p (c i j) -> p c j i", i=4, j=4),
                 w4_raw[b][:].rearrange("p j (c i) -> p c j i", i=4),
@@ -169,7 +172,7 @@ def tile_list_sumo_bout_features_kernel(
             cols = slice(P * t, P * (t + 1))
             for half in range(2):
                 picked = slice(BANK * half, BANK * (half + 1))
-                bank = ps1.tile([P, BANK], F32, name="bank")
+                bank = psum.tile([P, BANK], F32, name="bank")
                 for a in range(2):
                     nc.tensor.matmul_mx(
                         out=bank[:],
@@ -182,129 +185,190 @@ def tile_list_sumo_bout_features_kernel(
                     )
                 nc.scalar.activation(window[:, picked], bank[:], func, bias=bias)
 
-        h1, h2, grip1, grip2, least, rows = {}, {}, {}, {}, {}, {}
+        h1, h2, grip1, grip2, least, bounded, rows = {}, {}, {}, {}, {}, {}, {}
 
         def make_h2(s):
-            h2[s] = ring.tile([P, S], F32, name="h2", bufs=4)
+            if s == 0:
+                h2[s] = ring.tile([P, S], F32, name="h2", tag="B", bufs=1, align_bytes=64)
+            else:
+                h2[s] = ring.tile([P, S], F32, name="h2", bufs=4)
             first_stage(w2c, w2s, s // 4, s % 4, h2[s], ACT.Silu, 0.0)
 
         def pick_h2(s):
-            grip2[s] = ring.tile([P, PAIRS], F32, name="grip2", bufs=6)
+            if s == 0:
+                grip2[s] = once([P, PAIRS], F32, "grip2", "I")
+            else:
+                grip2[s] = ring.tile([P, PAIRS], F32, name="grip2", bufs=6)
             nc.vector.tensor_copy(grip2[s][:], h2[s][:].indirect(pos2_t[:]))
 
         def make_h1(s):
-            h1[s] = ring.tile([P, S], F32, name="h1", bufs=5)
+            if s == 0:
+                h1[s] = once([P, S], F32, "h1", "A")
+            else:
+                h1[s] = ring.tile([P, S], F32, name="h1", bufs=5)
             first_stage(w1c, w1s, s // 4, s % 4, h1[s], ACT.Identity, b1t[:, s // 4, s % 4 : s % 4 + 1])
 
         def pick_h1(s):
-            grip1[s] = ring.tile([P, PAIRS], F32, name="grip1", bufs=4)
-            nc.vector.tensor_copy(grip1[s][:], h1[s][:].indirect(pos2_t[:]))
-            charge = ring.tile([P, PAIRS], F32, name="charge", bufs=2)
-            nc.vector.tensor_copy(charge[:], h1[s][:].indirect(pos1_t[:]))
-            least[s] = ring.tile([P, PAIRS], F32, name="least", bufs=4)
-            nc.vector.tensor_tensor(least[s][:], charge[:], grip2[s][:], ALU.min)
-
-        def features(s, z_on_vector=False):
             b, t = s // 4, s % 4
             if t == 0:
-                rows[("z", b)] = ring.tile([P, PACK, PAIRS], BF16, name="zrows")
-                rows[("x", b)] = ring.tile([P, PACK, PAIRS], BF16, name="xrows")
-            bounded = ring.tile([P, PAIRS], F32, name="bounded", bufs=2)
-            nc.scalar.activation(bounded[:], grip1[s][:], ACT.Tanh)
-            nc.scalar.activation(rows[("x", b)][:, t, :], bounded[:], ACT.Copy, scale=gtt[:, b, t : t + 1])
-            if z_on_vector:
-                nc.vector.tensor_scalar(rows[("z", b)][:, t, :], least[s][:], gzt[:, b, t : t + 1], None, ALU.mult)
+                least[b] = ring.tile([P, PACK, PAIRS], F32, name="least")
+            behind = {2: "after_w1_1", 6: "after_w4_0", 7: "after_w4_1"}
+            if s in behind:
+                charge = once([P, PAIRS], F32, "charge", behind[s])
             else:
-                nc.scalar.activation(rows[("z", b)][:, t, :], least[s][:], ACT.Copy, scale=gzt[:, b, t : t + 1])
+                charge = ring.tile([P, PAIRS], F32, name="charge", bufs=2)
+            nc.vector.tensor_copy(charge[:], h1[s][:].indirect(pos1_t[:]))
+            behind = {2: "after_w1_0", 7: "woven_x0"}
+            if s in behind:
+                grip1[s] = once([P, PAIRS], F32, "grip1", behind[s])
+            else:
+                grip1[s] = ring.tile([P, PAIRS], F32, name="grip1", bufs=4)
+            nc.vector.tensor_copy(grip1[s][:], h1[s][:].indirect(pos2_t[:]))
+            nc.vector.tensor_tensor(least[b][:, t, :], charge[:], grip2[s][:], ALU.min)
 
-        acc = [ps2.tile([P, PAIRS], F32, name="acc%d" % j) for j in range(4)]
+        def bound(s):
+            if s % 4 == 0:
+                bounded[s // 4] = once([P, PACK, PAIRS], F32, "bounded", ("B", "bounded")[s // 4])
+            nc.scalar.activation(bounded[s // 4][:, s % 4, :], grip1[s][:], ACT.Tanh)
 
-        def second_stage(kind, b, first, last, on_vector):
-            grouped = ring.tile([P, PAIRS * PACK], BF16, name="fg", tag="fgrouped%d" % b, bufs=2 - b, align_bytes=64)
+        def scale_rows(kind, s):
+            b, t = s // 4, s % 4
+            if t == 0:
+                rows[(kind, b)] = once([P, PACK, PAIRS], BF16, kind + "rows", {"z": "A", "x": "xrows"}[kind])
+            src, gain = {"z": (least, gzt), "x": (bounded, gtt)}[kind]
+            nc.scalar.activation(rows[(kind, b)][:, t, :], src[b][:, t, :], ACT.Copy, scale=gain[:, b, t : t + 1])
+
+        acc = {}
+        HALF = PAIRS // 2
+
+        def weave(kind, b, m0, width, how):
+            grouped = once([P, width * PACK], BF16, "fg", "woven_z" if kind == "z" else "woven_x%d" % b)
             dst = grouped[:].rearrange("p (c i t) -> p c t i", i=4, t=4)
-            src = rows[(kind, b)][:].rearrange("p t (c i) -> p c t i", i=4)
-            if on_vector:
-                nc.vector.tensor_copy(dst, src)
-            else:
-                nc.scalar.copy(dst, src)
-            codes, scales = quantise(grouped, "%sq%d" % (kind, b))
-            for j in range(4):
-                cols = slice(P * j, P * (j + 1))
-                if kind == "z":
-                    lhs = w3["w"][:, b, 2 * P * j : 2 * P * (j + 1)].bitcast(FP4X4)
-                    lhs_scale = w3["s"][:, b, cols]
-                else:
-                    lhs = w4c[b][:, cols].bitcast(FP8X4)
-                    lhs_scale = w4s[b][:, cols]
-                nc.tensor.matmul_mx(
-                    out=acc[j][:], lhsT=lhs, lhsT_scale=lhs_scale, rhs=codes.bitcast(FP8X4), rhs_scale=scales,
-                    start=first, stop=last,
+            if how == "fused":
+                src, gain = {"z": (least, gzt), "x": (bounded, gtt)}[kind]
+                nc.vector.tensor_tensor(
+                    dst,
+                    src[b][:, :, m0 : m0 + width].rearrange("p t (c i) -> p c t i", i=4),
+                    gain[:, b, :].unsqueeze(1).unsqueeze(3).to_broadcast([P, width // 4, PACK, 4]),
+                    ALU.mult,
                 )
+            elif how == "vector":
+                nc.vector.tensor_copy(dst, rows[(kind, b)][:, :, m0 : m0 + width].rearrange("p t (c i) -> p c t i", i=4))
+            else:
+                nc.scalar.copy(dst, rows[(kind, b)][:, :, m0 : m0 + width].rearrange("p t (c i) -> p c t i", i=4))
+            return grouped
+
+        def second_stage(kind, b, m0, grouped, first, last):
+            width = grouped.shape[1] // PACK
+            codes = keep.tile([P, width], U32, name="%sc%d_%d" % (kind, b, m0), align_bytes=64)
+            scales = keep.tile([P, width], U8, name="%ss%d_%d" % (kind, b, m0), align_bytes=64)
+            nc.vector.quantize_mx(out=codes[:].bitcast(FP8X4), scales=scales[:], in_=grouped[:])
+            step = P if kind == "z" else HALF
+            for half in range(m0 // HALF, (m0 + width) // HALF):
+                for j in range(4):
+                    if first:
+                        acc[(half, j)] = psum.tile([P, HALF], F32, name="acc", tag="bank")
+                    cols = slice(P * j, P * (j + 1))
+                    if kind == "z":
+                        lhs = w3["w"][:, b, 2 * P * j : 2 * P * (j + 1)].bitcast(FP4X4)
+                        lhs_scale = w3["s"][:, b, cols]
+                    else:
+                        lhs = w4c[b][:, cols].bitcast(FP8X4)
+                        lhs_scale = w4s[b][:, cols]
+                    for c0 in range(0, HALF, step):
+                        mine = slice(HALF * half - m0 + c0, HALF * half - m0 + c0 + step)
+                        nc.tensor.matmul_mx(
+                            out=acc[(half, j)][:, c0 : c0 + step],
+                            lhsT=lhs,
+                            lhsT_scale=lhs_scale,
+                            rhs=codes[:, mine].bitcast(FP8X4),
+                            rhs_scale=scales[:, mine],
+                            start=first and c0 == 0,
+                            stop=last and c0 + step == HALF,
+                        )
+
+        def store(half, on_vector):
+            for j in range(4):
+                res = ring.tile([P, HALF], F32, name="res", bufs=8)
+                if j in on_vector:
+                    nc.vector.tensor_copy(res[:], acc[(half, j)][:])
+                else:
+                    nc.scalar.copy(res[:], acc[(half, j)][:])
+                nc.sync.dma_start(out[P * j : P * (j + 1), HALF * half : HALF * (half + 1)], res[:])
 
         deal_w2(0)
-        load_w3()
+        load_w2(1, "E")
         prep_w1(0, 0, False)
-        load_w2(1, "rawA", 1)
+        gather_second_pass()
+        load_w3()
         make_h2(0)
         prep_w1(1, 0, True)
-        load_w1(0, 1, "rawB", 1)
+        load_w1(1, 1, "C")
         make_h2(1)
         pick_h2(0)
+        load_w1(0, 1, "B")
         make_h2(2)
         make_h1(0)
         make_h2(3)
         pick_h2(1)
-        deal_w2(1)
-        load_w1(1, 1, "rawA", 1)
-        load_w3_scales()
         make_h1(1)
         pick_h2(2)
+        deal_w2(1)
+        w3["s"] = load_scale_rows(nc.sync, w3_scales, N, "w3s", "E")
         pick_h1(0)
+        load_w4(0, "A")
         make_h1(2)
         make_h1(3)
         pick_h2(3)
         prep_w1(0, 1, False)
-        load_w4(0, "rawB", 1)
         prep_w1(1, 1, False)
-        load_w4(1, "rawA", 1)
+        load_w4(1, "C")
         pick_h1(1)
         make_h2(4)
-        features(0)
+        bound(0)
         make_h2(5)
         pick_h1(2)
-        features(1)
         make_h2(6)
+        bound(1)
         make_h2(7)
         pick_h1(3)
         make_h1(4)
-        features(2)
+        bound(2)
         pick_h2(4)
         pick_h2(5)
         make_h1(5)
-        features(3)
+        bound(3)
         pick_h2(6)
         pick_h2(7)
-        make_h1(6)
+        scale_rows("x", 0)
+        scale_rows("x", 1)
+        scale_rows("x", 2)
+        scale_rows("x", 3)
         pick_h1(4)
-        make_h1(7)
         prep_w4(0)
+        make_h1(6)
         pick_h1(5)
-        second_stage("z", 0, True, False, False)
-        features(4)
-        prep_w4(1)
+        make_h1(7)
+        x0 = weave("x", 0, 0, PAIRS, "scalar")
         pick_h1(6)
-        second_stage("x", 0, False, False, True)
-        features(5)
+        second_stage("x", 0, 0, x0, True, False)
+        prep_w4(1)
+        scale_rows("z", 0)
+        scale_rows("z", 1)
+        scale_rows("z", 2)
+        scale_rows("z", 3)
         pick_h1(7)
-        features(6, True)
-        features(7, True)
-        second_stage("z", 1, False, False, True)
-        second_stage("x", 1, False, True, True)
-
-        for j in range(4):
-            res = ring.tile([P, PAIRS], F32, name="res", tag="grip2", bufs=6)
-            if j % 2 == 0:
-                nc.scalar.copy(res[:], acc[j][:])
-            else:
-                nc.vector.tensor_copy(res[:], acc[j][:])
-            nc.sync.dma_start(out[P * j : P * (j + 1), :], res[:])
+        z0 = weave("z", 0, 0, PAIRS, "scalar")
+        bound(4)
+        bound(5)
+        bound(6)
+        bound(7)
+        z1 = weave("z", 1, 0, PAIRS, "fused")
+        second_stage("z", 0, 0, z0, False, False)
+        second_stage("z", 1, 0, z1, False, False)
+        x1a = weave("x", 1, 0, HALF, "fused")
+        second_stage("x", 1, 0, x1a, False, True)
+        x1b = weave("x", 1, HALF, HALF, "fused")
+        store(0, ())
+        second_stage("x", 1, HALF, x1b, False, True)
+        store(1, (1, 3))

@@ -18,8 +18,13 @@ ALU = mybir.AluOpType
 
 P = 128
 PACK = 4
-KP = P * PACK
+PASS = P * PACK
 BANK = 512
+HALF = PAIRS // 2
+SLICES = H // P
+SCALE_ROWS = 32
+LIST_ROWS = 16
+H1_TILES, H2_TILES = 4, 4
 
 
 def tile_list_sumo_bout_features_kernel(
@@ -29,346 +34,300 @@ def tile_list_sumo_bout_features_kernel(
     with ExitStack() as ctx:
         lists = ctx.enter_context(tc.tile_pool(name="lists", bufs=1))
         keep = ctx.enter_context(tc.tile_pool(name="keep", bufs=1))
-        ring = ctx.enter_context(tc.tile_pool(name="ring", bufs=2))
+        work = ctx.enter_context(tc.tile_pool(name="work", bufs=1))
         psum = ctx.enter_context(tc.psum_pool(name="psum", bufs=8))
 
-        w2_all = w2_words.rearrange("a p c i -> p a (c i)").bitcast(I32)
-        w2_raw, w1_raw, w4_raw, w3, w2c, w2s = {}, {}, {}, {}, {}, {}
+        def in_slot(slot, shape, dtype, name):
+            return work.tile(shape, dtype, name=name, tag=slot, align_bytes=64)
 
-        def once(shape, dtype, name, slot):
-            return ring.tile(shape, dtype, name=name, tag=slot, bufs=1, align_bytes=64)
+        def load_list(entries, name):
+            offsets = lists.tile(list(entries.shape), U16, name=name)
+            nc.sync.dma_start(offsets[:], entries)
+            return offsets
 
-        def load_table(a, slot):
-            words = once([P, T], U16, "tw%d" % a, slot)
+        def load_scale_rows(scales, slot, name):
+            rows = in_slot(slot, [P, scales.shape[2]], U8, name)
+            nc.sync.dma_start(rows[0:SCALE_ROWS, :].bitcast(I32), scales.rearrange("a q c -> q a c").bitcast(I32))
+            nc.vector.memset(rows[SCALE_ROWS:64, :].bitcast(I32), 0)
+            nc.vector.memset(rows[64:P, :].bitcast(I32), 0)
+            return rows
+
+        def zeroed_planes(tile, engine):
+            engine.memset(tile[:].bitcast(I32), 0)
+            return tile
+
+        def spread_scale_rows(queue, planes, rows):
+            for quad in range(4):
+                queue.dma_start(
+                    planes[32 * quad : 32 * quad + 4, :, :].bitcast(I32), rows[8 * quad : 8 * quad + 8, :].bitcast(I32)
+                )
+
+        def load_table_words(a, slot):
+            words = in_slot(slot, [P, T], U16, "table_words%d" % a)
             nc.sync.dma_start(words[:].bitcast(I32), tab_words[a].bitcast(I32))
             return words
 
-        def load_w2(b, slot):
-            w2_raw[b] = once([P, 2, KP], I32, "w2raw%d" % b, slot)
-            nc.sync.dma_start(w2_raw[b][:], w2_all[:, :, KP * b : KP * (b + 1)])
+        def load_w2_words(b, slot):
+            words = in_slot(slot, [P, 2, PASS], I32, "w2_words%d" % b)
+            both_passes = w2_words.rearrange("a p c i -> p a (c i)").bitcast(I32)
+            nc.sync.dma_start(words[:], both_passes[:, :, PASS * b : PASS * (b + 1)])
+            return words
+
+        def load_rows(rows, slot, name):
+            raw = in_slot(slot, [P, PACK, rows.shape[1]], F32, name)
+            nc.sync.dma_start(raw[:], rows.rearrange("(p j) c -> p j c", j=PACK))
+            return raw
 
         def load_w1(a, b, slot):
-            w1_raw[(a, b)] = once([P, PACK, KP], F32, "w1raw%d%d" % (a, b), slot)
-            nc.sync.dma_start(
-                w1_raw[(a, b)][:],
-                w1[KP * a : KP * (a + 1), KP * b : KP * (b + 1)].rearrange("(p j) c -> p j c", j=PACK),
-            )
+            return load_rows(w1[PASS * a : PASS * (a + 1), PASS * b : PASS * (b + 1)], slot, "w1_%d%d" % (a, b))
 
         def load_w4(b, slot):
-            w4_raw[b] = once([P, PACK, N], F32, "w4raw%d" % b, slot)
-            nc.sync.dma_start(w4_raw[b][:], w4[KP * b : KP * (b + 1), :].rearrange("(p j) n -> p j n", j=PACK))
+            return load_rows(w4[PASS * b : PASS * (b + 1), :], slot, "w4_%d" % b)
 
-        def load_scale_rows(queue, scales, width, name, slot):
-            plane = once([P, 2, width], U8, name, slot)
-            nc.gpsimd.memset(plane[:].bitcast(I32), 0)
-            for q in range(4):
-                queue.dma_start(
-                    plane[32 * q : 32 * q + 4, :, :].bitcast(I32),
-                    scales[:, 4 * q : 4 * q + 4, :].rearrange("a r c -> r a c").bitcast(I32),
-                )
-            return plane
+        def quantise(woven, name):
+            width = woven.shape[1] // PACK
+            codes = keep.tile([P, width], U32, name=name + "_codes", align_bytes=64)
+            plane = keep.tile([P, width], U8, name=name + "_plane", align_bytes=64)
+            nc.vector.quantize_mx(out=codes[:].bitcast(FP8X4), scales=plane[:], in_=woven[:])
+            return codes[:], plane[:]
 
-        offs_t = lists.tile([P, S // 16], U16, name="offs_t")
-        nc.sync.dma_start(offs_t[:], offs)
-        w2s_raw = once([P, H], U8, "w2s_raw", "F")
-        nc.sync.dma_start(w2s_raw[0:32, :].bitcast(I32), w2_scales.rearrange("a q c -> q a c").bitcast(I32))
-        tsc = once([P, T], U8, "tsc", "A")
-        nc.sync.dma_start(tsc[0:32, :].bitcast(I32), tab_scales.rearrange("a q t -> q a t").bitcast(I32))
-        for rows_tile in (w2s_raw, tsc):
-            nc.vector.memset(rows_tile[32:64, :].bitcast(I32), 0)
-            nc.vector.memset(rows_tile[64:P, :].bitcast(I32), 0)
-        pos2_t = lists.tile([P, PAIRS // 16], U16, name="pos2_t")
-        nc.sync.dma_start(pos2_t[:], pos2)
-        pos1_t = lists.tile([P, PAIRS // 16], U16, name="pos1_t")
-        nc.sync.dma_start(pos1_t[:], pos1)
-        b1t = keep.tile([P, 2, PACK], F32, name="b1t")
-        nc.sync.dma_start(b1t[:], b1.rearrange("(b p t) -> p b t", b=2, t=PACK))
-        tw0 = load_table(0, "C")
-        load_w1(0, 0, "B")
-        load_w2(0, "E")
-        tw1 = load_table(1, "G")
-        warm = keep.tile([P, 8], F32, name="warm")
-        nc.gpsimd.memset(warm[:, 0:4], 0.0)
-        nc.scalar.activation(warm[:, 4:8], warm[:, 0:4], ACT.Silu)
-        w2plane = keep.tile([P, 2, H], U8, name="w2plane", align_bytes=64)
-        nc.gpsimd.memset(w2plane[:].bitcast(I32), 0)
-        tplane = keep.tile([P, 2, S], U8, name="tplane", align_bytes=64)
-        nc.vector.memset(tplane[:].bitcast(I32), 0)
+        w1q, w2q, w4q = {}, {}, {}
 
-        def spread_rows(queues, plane, rows_tile):
-            for q, queue in enumerate(queues):
-                queue.dma_start(
-                    plane[32 * q : 32 * q + 4, :, :].bitcast(I32), rows_tile[8 * q : 8 * q + 8, :].bitcast(I32)
-                )
+        def quantise_w1(a, b, raw, copy, slot):
+            woven = in_slot(slot, [P, PASS * PACK], BF16, "w1_woven")
+            copy(
+                woven[:].rearrange("p (t m j) -> p m j t", t=PACK, j=PACK),
+                raw[:].rearrange("p j (m t) -> p m j t", t=PACK),
+            )
+            w1q[(a, b)] = quantise(woven, "w1_%d%d" % (a, b))
 
-        w2s_dealt = once([P, H], U8, "w2s_dealt", "H")
-        nc.vector.tensor_copy(
-            w2s_dealt[:].rearrange("p (b t c i) -> p b c t i", b=2, t=4, i=16),
-            w2s_raw[:].rearrange("p (b c i t) -> p b c t i", b=2, t=4, i=16),
-        )
-        spread_rows((nc.gpsimd,) * 4, w2plane, w2s_dealt)
-        gains = once([P, 2, 2, PACK], F32, "gains", "H")
-        for i, vec in enumerate((gz, gt)):
-            nc.gpsimd.dma_start(gains[:, i, :, :], vec.rearrange("(b p t) -> p b t", b=2, t=PACK))
-        gzt, gtt = gains[:, 0, :, :], gains[:, 1, :, :]
+        def quantise_w4(b, raw):
+            woven = in_slot("w4_woven", [P, N * PACK], BF16, "w4_woven")
+            nc.scalar.copy(
+                woven[:].rearrange("p (c i j) -> p c j i", i=4, j=PACK),
+                raw[:].rearrange("p j (c i) -> p c j i", i=4),
+            )
+            w4q[b] = quantise(woven, "w4_%d" % b)
 
-        gsc = once([P, S], U8, "gsc", "D")
-        nc.vector.tensor_copy(gsc[:], tsc[:].indirect(offs_t[:]))
-        spread_rows((nc.scalar,) * 4, tplane, gsc)
-        planes = [tplane[:, 0, :], tplane[:, 1, :]]
-        gw = [keep.tile([P, S], U16, name="gw%d" % a, align_bytes=64) for a in range(2)]
-        nc.vector.tensor_copy(gw[0][:], tw0[:].indirect(offs_t[:]))
-        load_w1(1, 0, "C")
-
-        def gather_second_pass():
-            for half in range(2):
-                nc.vector.tensor_copy(
-                    gw[1][:, BANK * half : BANK * (half + 1)], tw1[:].indirect(offs_t[:, 32 * half : 32 * (half + 1)])
-                )
-
-        def load_w3():
-            w3["w"] = once([P, 2, 2 * N], U8, "w3w", "G")
-            nc.sync.dma_start(w3["w"][:].bitcast(I32), w3_words.rearrange("a p c -> p a c").bitcast(I32))
-
-        def deal_w2(b):
-            codes = keep.tile([P, 2, KP], I32, name="w2c%d" % b, align_bytes=64)
+        def deal_w2_words(b, raw):
+            codes = keep.tile([P, 2, PASS], I32, name="w2_codes%d" % b, align_bytes=64)
             nc.vector.tensor_copy(
-                codes[:].rearrange("p a (t c i) -> p a c t i", t=4, i=4),
-                w2_raw[b][:].rearrange("p a (c i t) -> p a c t i", t=4, i=4),
+                codes[:].rearrange("p a (t c i) -> p a c t i", t=PACK, i=4),
+                raw[:].rearrange("p a (c i t) -> p a c t i", t=PACK, i=4),
             )
             for a in range(2):
-                w2c[(a, b)] = codes[:, a, :]
-                w2s[(a, b)] = w2plane[:, a, KP * b : KP * (b + 1)]
+                w2q[(a, b)] = (codes[:, a, :], w2_planes[:, a, PASS * b : PASS * (b + 1)])
 
-        w1c, w1s = {}, {}
+        offs_t = load_list(offs, "offs")
+        w2_rows = load_scale_rows(w2_scales, "w2_rows", "w2_rows")
+        table_rows = load_scale_rows(tab_scales, "slot_a", "table_rows")
+        pos2_t = load_list(pos2, "pos2")
+        pos1_t = load_list(pos1, "pos1")
+        table0 = load_table_words(0, "slot_b")
+        w1_00 = load_w1(0, 0, "slot_c")
+        w2_words0 = load_w2_words(0, "slot_h")
+        zero = keep.tile([P, 2], F32, name="zero")
+        nc.gpsimd.memset(zero[:, 0:1], 0.0)
+        nc.scalar.activation(zero[:, 1:2], zero[:, 0:1], ACT.Silu)
+        w2_planes = zeroed_planes(keep.tile([P, 2, H], U8, name="w2_planes", align_bytes=64), nc.gpsimd)
+        vectors = keep.tile([P, 3, 2, PACK], F32, name="vectors")
+        for i, vector in enumerate((b1, gz, gt)):
+            nc.gpsimd.dma_start(vectors[:, i, :, :], vector.rearrange("(b p t) -> p b t", b=2, t=PACK))
+        bias = vectors[:, 0, :, :]
+        gain = {"z": vectors[:, 1, :, :], "x": vectors[:, 2, :, :]}
+        table_planes = zeroed_planes(keep.tile([P, 2, S], U8, name="table_planes", align_bytes=64), nc.vector)
 
-        def quantise(grouped, name):
-            codes = keep.tile([P, KP], U32, name=name + "c", align_bytes=64)
-            scales = keep.tile([P, KP], U8, name=name + "s", align_bytes=64)
-            nc.vector.quantize_mx(out=codes[:].bitcast(FP8X4), scales=scales[:], in_=grouped[:])
-            return codes[:], scales[:]
+        w2_rows_dealt = keep.tile([P, H], U8, name="w2_rows_dealt", align_bytes=64)
+        nc.vector.tensor_copy(
+            w2_rows_dealt[:].rearrange("p (b t c i) -> p b c t i", b=2, t=PACK, i=16),
+            w2_rows[:].rearrange("p (b c i t) -> p b c t i", b=2, t=PACK, i=16),
+        )
+        spread_scale_rows(nc.scalar, w2_planes, w2_rows_dealt)
 
-        def prep_w1(a, b, on_vector):
-            grouped = once([P, KP * PACK], BF16, "wg", (("first", "I"), ("after_w1_0", "after_w1_1"))[b][a])
-            dst = grouped[:].rearrange("p (t m j) -> p m t j", t=4, j=4)
-            src = w1_raw[(a, b)][:].rearrange("p j (m t) -> p m t j", t=4)
-            if on_vector:
-                nc.vector.tensor_copy(dst, src)
-            else:
-                nc.scalar.copy(dst, src)
-            w1c[(a, b)], w1s[(a, b)] = quantise(grouped, "w1q%d%d" % (a, b))
+        picked_rows = keep.tile([P, S], U8, name="picked_rows", align_bytes=64)
+        nc.vector.tensor_copy(picked_rows[:], table_rows[:].indirect(offs_t[:]))
+        table1 = load_table_words(1, "slot_a")
+        spread_scale_rows(nc.sync, table_planes, picked_rows)
+        picked = [keep.tile([P, S], U16, name="picked%d" % a, align_bytes=64) for a in range(2)]
+        nc.vector.tensor_copy(picked[0][:], table0[:].indirect(offs_t[:]))
+        w1_10 = load_w1(1, 0, "slot_b")
+        deal_w2_words(0, w2_words0)
+        w2_words1 = load_w2_words(1, "slot_h")
+        quantise_w1(0, 0, w1_00, nc.scalar.copy, "slot_d")
+        for c0 in range(0, S, BANK):
+            entries = offs_t[:, c0 // LIST_ROWS : (c0 + BANK) // LIST_ROWS]
+            nc.vector.tensor_copy(picked[1][:, c0 : c0 + BANK], table1[:].indirect(entries))
+        w3_codes = in_slot("slot_d", [P, 2, 2 * N], U8, "w3_codes")
+        nc.sync.dma_start(w3_codes[:].bitcast(I32), w3_words.rearrange("a p c -> p a c").bitcast(I32))
 
-        w4c, w4s = {}, {}
+        grip2 = {}
+        grip1 = {}
+        unscaled = {}
 
-        def prep_w4(b):
-            grouped = once([P, N * PACK], BF16, "wg", "after_w4_%d" % b)
-            nc.scalar.copy(
-                grouped[:].rearrange("p (c i j) -> p c j i", i=4, j=4),
-                w4_raw[b][:].rearrange("p j (c i) -> p c j i", i=4),
-            )
-            w4c[b], w4s[b] = quantise(grouped, "w4q%d" % b)
-
-        def first_stage(codes, scales, b, t, window, func, bias):
+        def first_stage(weights, s, window, func, slice_bias):
+            b, t = divmod(s, PACK)
             cols = slice(P * t, P * (t + 1))
-            for half in range(2):
-                picked = slice(BANK * half, BANK * (half + 1))
+            for c0 in range(0, S, BANK):
                 bank = psum.tile([P, BANK], F32, name="bank")
                 for a in range(2):
+                    codes, plane = weights[(a, b)]
                     nc.tensor.matmul_mx(
                         out=bank[:],
-                        lhsT=codes[(a, b)][:, cols].bitcast(FP8X4),
-                        lhsT_scale=scales[(a, b)][:, cols],
-                        rhs=gw[a][:, picked].bitcast(FP4X4),
-                        rhs_scale=planes[a][:, picked],
+                        lhsT=codes[:, cols].bitcast(FP8X4),
+                        lhsT_scale=plane[:, cols],
+                        rhs=picked[a][:, c0 : c0 + BANK].bitcast(FP4X4),
+                        rhs_scale=table_planes[:, a, c0 : c0 + BANK],
                         start=(a == 0),
                         stop=(a == 1),
                     )
-                nc.scalar.activation(window[:, picked], bank[:], func, bias=bias)
+                nc.scalar.activation(window[:, c0 : c0 + BANK], bank[:], func, bias=slice_bias)
 
-        h1, h2, grip1, grip2, least, bounded, rows = {}, {}, {}, {}, {}, {}, {}
+        def tile_for(name, shape, bufs, slot):
+            if slot is None:
+                return work.tile(shape, F32, name=name, bufs=bufs)
+            return in_slot(slot, shape, F32, name)
 
-        def make_h2(s):
-            if s == 0:
-                h2[s] = ring.tile([P, S], F32, name="h2", tag="B", bufs=1, align_bytes=64)
-            else:
-                h2[s] = ring.tile([P, S], F32, name="h2", bufs=4)
-            first_stage(w2c, w2s, s // 4, s % 4, h2[s], ACT.Silu, 0.0)
+        def make_h2(s, window_slot=None):
+            h2 = tile_for("h2", [P, S], H2_TILES, window_slot)
+            first_stage(w2q, s, h2, ACT.Silu, zero[:, 1:2])
+            return h2
 
-        def pick_h2(s):
-            if s == 0:
-                grip2[s] = once([P, PAIRS], F32, "grip2", "I")
-            else:
-                grip2[s] = ring.tile([P, PAIRS], F32, name="grip2", bufs=6)
-            nc.vector.tensor_copy(grip2[s][:], h2[s][:].indirect(pos2_t[:]))
+        def pick_h2(s, h2):
+            b, t = divmod(s, PACK)
+            nc.vector.tensor_copy(grip2[b][:, t, :], h2[:].indirect(pos2_t[:]))
 
-        def make_h1(s):
-            if s == 0:
-                h1[s] = once([P, S], F32, "h1", "A")
-            else:
-                h1[s] = ring.tile([P, S], F32, name="h1", bufs=5)
-            first_stage(w1c, w1s, s // 4, s % 4, h1[s], ACT.Identity, b1t[:, s // 4, s % 4 : s % 4 + 1])
+        def h2_slice(s):
+            pick_h2(s, make_h2(s))
 
-        def pick_h1(s):
-            b, t = s // 4, s % 4
+        def h1_slice(s, window_slot=None, grip_slot=None):
+            b, t = divmod(s, PACK)
+            h1 = tile_for("h1", [P, S], H1_TILES, window_slot)
+            first_stage(w1q, s, h1, ACT.Identity, bias[:, b, t : t + 1])
+            charge = work.tile([P, PAIRS], F32, name="charge", bufs=2)
+            nc.vector.tensor_copy(charge[:], h1[:].indirect(pos1_t[:]))
+            grip1[s] = tile_for("grip1", [P, PAIRS], PACK, grip_slot)
+            nc.vector.tensor_copy(grip1[s][:], h1[:].indirect(pos2_t[:]))
             if t == 0:
-                least[b] = ring.tile([P, PACK, PAIRS], F32, name="least")
-            behind = {2: "after_w1_1", 6: "after_w4_0", 7: "after_w4_1"}
-            if s in behind:
-                charge = once([P, PAIRS], F32, "charge", behind[s])
-            else:
-                charge = ring.tile([P, PAIRS], F32, name="charge", bufs=2)
-            nc.vector.tensor_copy(charge[:], h1[s][:].indirect(pos1_t[:]))
-            behind = {2: "after_w1_0", 7: "woven_x0"}
-            if s in behind:
-                grip1[s] = once([P, PAIRS], F32, "grip1", behind[s])
-            else:
-                grip1[s] = ring.tile([P, PAIRS], F32, name="grip1", bufs=4)
-            nc.vector.tensor_copy(grip1[s][:], h1[s][:].indirect(pos2_t[:]))
-            nc.vector.tensor_tensor(least[b][:, t, :], charge[:], grip2[s][:], ALU.min)
+                unscaled[("z", b)] = work.tile([P, PACK, PAIRS], F32, name="least", bufs=2)
+            nc.vector.tensor_tensor(unscaled[("z", b)][:, t, :], charge[:], grip2[b][:, t, :], ALU.min)
 
         def bound(s):
-            if s % 4 == 0:
-                bounded[s // 4] = once([P, PACK, PAIRS], F32, "bounded", ("B", "bounded")[s // 4])
-            nc.scalar.activation(bounded[s // 4][:, s % 4, :], grip1[s][:], ACT.Tanh)
+            b, t = divmod(s, PACK)
+            nc.scalar.activation(unscaled[("x", b)][:, t, :], grip1[s][:], ACT.Tanh)
 
-        def scale_rows(kind, s):
-            b, t = s // 4, s % 4
-            if t == 0:
-                rows[(kind, b)] = once([P, PACK, PAIRS], BF16, kind + "rows", {"z": "A", "x": "xrows"}[kind])
-            src, gain = {"z": (least, gzt), "x": (bounded, gtt)}[kind]
-            nc.scalar.activation(rows[(kind, b)][:, t, :], src[b][:, t, :], ACT.Copy, scale=gain[:, b, t : t + 1])
+        def scale_slice(rows, kind, s):
+            b, t = divmod(s, PACK)
+            nc.scalar.activation(rows[:, t, :], unscaled[(kind, b)][:, t, :], ACT.Copy, scale=gain[kind][:, b, t : t + 1])
 
-        acc = {}
-        HALF = PAIRS // 2
+        def by_fours(rows):
+            return rows.rearrange("p t (c i) -> p c t i", i=4)
 
-        def weave(kind, b, m0, width, how):
-            grouped = once([P, width * PACK], BF16, "fg", "woven_z" if kind == "z" else "woven_x%d" % b)
-            dst = grouped[:].rearrange("p (c i t) -> p c t i", i=4, t=4)
-            if how == "fused":
-                src, gain = {"z": (least, gzt), "x": (bounded, gtt)}[kind]
-                nc.vector.tensor_tensor(
-                    dst,
-                    src[b][:, :, m0 : m0 + width].rearrange("p t (c i) -> p c t i", i=4),
-                    gain[:, b, :].unsqueeze(1).unsqueeze(3).to_broadcast([P, width // 4, PACK, 4]),
-                    ALU.mult,
-                )
-            elif how == "vector":
-                nc.vector.tensor_copy(dst, rows[(kind, b)][:, :, m0 : m0 + width].rearrange("p t (c i) -> p c t i", i=4))
-            else:
-                nc.scalar.copy(dst, rows[(kind, b)][:, :, m0 : m0 + width].rearrange("p t (c i) -> p c t i", i=4))
-            return grouped
+        def woven_tile(width, slot):
+            woven = in_slot(slot, [P, width * PACK], BF16, "woven")
+            return woven, woven[:].rearrange("p (c i t) -> p c t i", i=4, t=PACK)
 
-        def second_stage(kind, b, m0, grouped, first, last):
-            width = grouped.shape[1] // PACK
-            codes = keep.tile([P, width], U32, name="%sc%d_%d" % (kind, b, m0), align_bytes=64)
-            scales = keep.tile([P, width], U8, name="%ss%d_%d" % (kind, b, m0), align_bytes=64)
-            nc.vector.quantize_mx(out=codes[:].bitcast(FP8X4), scales=scales[:], in_=grouped[:])
+        def weave(rows, slot):
+            woven, view = woven_tile(rows.shape[2], slot)
+            nc.scalar.copy(view, by_fours(rows))
+            return woven
+
+        def scale_and_weave(kind, b, m0, slot):
+            woven, view = woven_tile(HALF, slot)
+            gains = gain[kind][:, b, :].unsqueeze(1).unsqueeze(3).to_broadcast([P, HALF // 4, PACK, 4])
+            nc.vector.tensor_tensor(view, by_fours(unscaled[(kind, b)][:, :, m0 : m0 + HALF]), gains, ALU.mult)
+            return woven
+
+        sums = {}
+
+        def add_pass(kind, b, operand, m0, h0, first=False, last=False):
+            codes, plane = operand
             step = P if kind == "z" else HALF
-            for half in range(m0 // HALF, (m0 + width) // HALF):
-                for j in range(4):
-                    if first:
-                        acc[(half, j)] = psum.tile([P, HALF], F32, name="acc", tag="bank")
-                    cols = slice(P * j, P * (j + 1))
-                    if kind == "z":
-                        lhs = w3["w"][:, b, 2 * P * j : 2 * P * (j + 1)].bitcast(FP4X4)
-                        lhs_scale = w3["s"][:, b, cols]
-                    else:
-                        lhs = w4c[b][:, cols].bitcast(FP8X4)
-                        lhs_scale = w4s[b][:, cols]
-                    for c0 in range(0, HALF, step):
-                        mine = slice(HALF * half - m0 + c0, HALF * half - m0 + c0 + step)
-                        nc.tensor.matmul_mx(
-                            out=acc[(half, j)][:, c0 : c0 + step],
-                            lhsT=lhs,
-                            lhsT_scale=lhs_scale,
-                            rhs=codes[:, mine].bitcast(FP8X4),
-                            rhs_scale=scales[:, mine],
-                            start=first and c0 == 0,
-                            stop=last and c0 + step == HALF,
-                        )
-
-        def store(half, on_vector):
-            for j in range(4):
-                res = ring.tile([P, HALF], F32, name="res", bufs=8)
-                if j in on_vector:
-                    nc.vector.tensor_copy(res[:], acc[(half, j)][:])
+            for j in range(N // P):
+                if first:
+                    sums[(h0, j)] = psum.tile([P, HALF], F32, name="sum", tag="bank")
+                cols = slice(P * j, P * (j + 1))
+                if kind == "z":
+                    lhs = w3_codes[:, b, 2 * P * j : 2 * P * (j + 1)].bitcast(FP4X4)
+                    lhs_plane = w3_planes[:, b, cols]
                 else:
-                    nc.scalar.copy(res[:], acc[(half, j)][:])
-                nc.sync.dma_start(out[P * j : P * (j + 1), HALF * half : HALF * (half + 1)], res[:])
+                    lhs = w4q[b][0][:, cols].bitcast(FP8X4)
+                    lhs_plane = w4q[b][1][:, cols]
+                for c0 in range(0, HALF, step):
+                    moving = slice(h0 - m0 + c0, h0 - m0 + c0 + step)
+                    nc.tensor.matmul_mx(
+                        out=sums[(h0, j)][:, c0 : c0 + step],
+                        lhsT=lhs,
+                        lhsT_scale=lhs_plane,
+                        rhs=codes[:, moving].bitcast(FP8X4),
+                        rhs_scale=plane[:, moving],
+                        start=first and c0 == 0,
+                        stop=last and c0 + step == HALF,
+                    )
 
-        deal_w2(0)
-        load_w2(1, "E")
-        prep_w1(0, 0, False)
-        gather_second_pass()
-        load_w3()
-        make_h2(0)
-        prep_w1(1, 0, True)
-        load_w1(1, 1, "C")
-        make_h2(1)
-        pick_h2(0)
-        load_w1(0, 1, "B")
-        make_h2(2)
-        make_h1(0)
-        make_h2(3)
-        pick_h2(1)
-        make_h1(1)
-        pick_h2(2)
-        deal_w2(1)
-        w3["s"] = load_scale_rows(nc.sync, w3_scales, N, "w3s", "E")
-        pick_h1(0)
-        load_w4(0, "A")
-        make_h1(2)
-        make_h1(3)
-        pick_h2(3)
-        prep_w1(0, 1, False)
-        prep_w1(1, 1, False)
-        load_w4(1, "C")
-        pick_h1(1)
-        make_h2(4)
-        bound(0)
-        make_h2(5)
-        pick_h1(2)
-        make_h2(6)
-        bound(1)
-        make_h2(7)
-        pick_h1(3)
-        make_h1(4)
-        bound(2)
-        pick_h2(4)
-        pick_h2(5)
-        make_h1(5)
-        bound(3)
-        pick_h2(6)
-        pick_h2(7)
-        scale_rows("x", 0)
-        scale_rows("x", 1)
-        scale_rows("x", 2)
-        scale_rows("x", 3)
-        pick_h1(4)
-        prep_w4(0)
-        make_h1(6)
-        pick_h1(5)
-        make_h1(7)
-        x0 = weave("x", 0, 0, PAIRS, "scalar")
-        pick_h1(6)
-        second_stage("x", 0, 0, x0, True, False)
-        prep_w4(1)
-        scale_rows("z", 0)
-        scale_rows("z", 1)
-        scale_rows("z", 2)
-        scale_rows("z", 3)
-        pick_h1(7)
-        z0 = weave("z", 0, 0, PAIRS, "scalar")
-        bound(4)
-        bound(5)
-        bound(6)
-        bound(7)
-        z1 = weave("z", 1, 0, PAIRS, "fused")
-        second_stage("z", 0, 0, z0, False, False)
-        second_stage("z", 1, 0, z1, False, False)
-        x1a = weave("x", 1, 0, HALF, "fused")
-        second_stage("x", 1, 0, x1a, False, True)
-        x1b = weave("x", 1, HALF, HALF, "fused")
-        store(0, ())
-        second_stage("x", 1, HALF, x1b, False, True)
-        store(1, (1, 3))
+        def store(h0, copies):
+            for j in range(N // P):
+                result = work.tile([P, HALF], F32, name="result", bufs=8)
+                copies[j % len(copies)](result[:], sums[(h0, j)][:])
+                nc.sync.dma_start(out[P * j : P * (j + 1), h0 : h0 + HALF], result[:])
+
+        h2_first = make_h2(0, "slot_c")
+        quantise_w1(1, 0, w1_10, nc.vector.tensor_copy, "slot_e")
+        w1_11 = load_w1(1, 1, "slot_b")
+        deal_w2_words(1, w2_words1)
+        grip2[0] = in_slot("slot_e", [P, PACK, PAIRS], F32, "grip2")
+        pick_h2(0, h2_first)
+        w1_01 = load_w1(0, 1, "slot_c")
+        h2_slice(1)
+        h2_slice(2)
+        h1_slice(0, window_slot="slot_f")
+        w4_0 = load_w4(0, "slot_f")
+        h2_slice(3)
+        w3_planes = zeroed_planes(in_slot("slot_h", [P, 2, N], U8, "w3_planes"), nc.gpsimd)
+        for quad in range(4):
+            nc.sync.dma_start(
+                w3_planes[32 * quad : 32 * quad + 4, :, :].bitcast(I32),
+                w3_scales[:, 4 * quad : 4 * quad + 4, :].rearrange("a r c -> r a c").bitcast(I32),
+            )
+        h1_slice(1, window_slot="slot_i")
+        w4_1 = load_w4(1, "slot_i")
+        for s in range(2, PACK):
+            h1_slice(s)
+
+        quantise_w1(0, 1, w1_01, nc.scalar.copy, "w1_woven_a")
+        quantise_w1(1, 1, w1_11, nc.scalar.copy, "w1_woven_b")
+        unscaled[("x", 0)] = in_slot("slot_c", [P, PACK, PAIRS], F32, "bounded")
+        grip2[1] = in_slot("grip2_1", [P, PACK, PAIRS], F32, "grip2")
+        for t in range(PACK - 1):
+            h2_slice(PACK + t)
+            bound(t)
+        h2_slice(SLICES - 1)
+        quantise_w4(0, w4_0)
+        bound(PACK - 1)
+
+        h1_slice(PACK)
+        h1_slice(PACK + 1)
+        x_rows = in_slot("slot_g", [P, PACK, PAIRS], BF16, "x_rows")
+        for s in range(PACK):
+            scale_slice(x_rows, "x", s)
+        x_woven = weave(x_rows[:], "x0_woven")
+        h1_slice(PACK + 2)
+        quantise_w4(1, w4_1)
+        h1_slice(PACK + 3, grip_slot="slot_g")
+        x0q = quantise(x_woven, "x0")
+        for h0 in (0, HALF):
+            add_pass("x", 0, x0q, 0, h0, first=True)
+        z_rows = in_slot("slot_b", [P, PACK, PAIRS], BF16, "z_rows")
+        for s in range(PACK):
+            scale_slice(z_rows, "z", s)
+        unscaled[("x", 1)] = in_slot("bounded1", [P, PACK, PAIRS], F32, "bounded")
+        for s in range(PACK, SLICES):
+            bound(s)
+        z0q = quantise(weave(z_rows[:], "z0_woven"), "z0")
+
+        for h0, copies in ((0, [nc.scalar.copy]), (HALF, [nc.scalar.copy, nc.vector.tensor_copy])):
+            z_woven = scale_and_weave("z", 1, h0, "slot_g")
+            x_woven = scale_and_weave("x", 1, h0, "x1_woven")
+            add_pass("z", 0, z0q, 0, h0)
+            add_pass("z", 1, quantise(z_woven, "z1_%d" % h0), h0, h0)
+            add_pass("x", 1, quantise(x_woven, "x1_%d" % h0), h0, h0, last=True)
+            store(h0, copies)

from contextlib import ExitStack

import concourse.mybir as mybir

K, T, S, PAIRS, H, N = 1024, 4096, 1024, 512, 1024, 512
FLOPS = 2 * 2 * K * H * S + 2 * 2 * H * N * PAIRS

F32 = mybir.dt.float32
BF16 = mybir.dt.bfloat16
I32 = mybir.dt.int32
U32 = mybir.dt.uint32
U16 = mybir.dt.uint16
U8 = mybir.dt.uint8
FP8X4 = mybir.dt.float8_e4m3fn_x4
FP4X4 = mybir.dt.float4_e2m1fn_x4
ACT = mybir.ActivationFunctionType
ALU = mybir.AluOpType

P = 128
PACK = 4
PASS = P * PACK
BANK = 512
HALF = PAIRS // 2
SLICES = H // P
SCALE_ROWS = 32
LIST_ROWS = 16
H1_TILES, H2_TILES = 4, 4


def tile_list_sumo_bout_features_kernel(
    tc, tab_words, tab_scales, offs, pos1, pos2, w1, b1, w2_words, w2_scales, gz, gt, w3_words, w3_scales, w4, out
):
    nc = tc.nc
    with ExitStack() as ctx:
        lists = ctx.enter_context(tc.tile_pool(name="lists", bufs=1))
        keep = ctx.enter_context(tc.tile_pool(name="keep", bufs=1))
        work = ctx.enter_context(tc.tile_pool(name="work", bufs=1))
        psum = ctx.enter_context(tc.psum_pool(name="psum", bufs=8))

        def in_slot(slot, shape, dtype, name):
            return work.tile(shape, dtype, name=name, tag=slot, align_bytes=64)

        def load_list(entries, name):
            offsets = lists.tile(list(entries.shape), U16, name=name)
            nc.sync.dma_start(offsets[:], entries)
            return offsets

        def load_scale_rows(scales, slot, name):
            rows = in_slot(slot, [P, scales.shape[2]], U8, name)
            nc.sync.dma_start(rows[0:SCALE_ROWS, :].bitcast(I32), scales.rearrange("a q c -> q a c").bitcast(I32))
            nc.vector.memset(rows[SCALE_ROWS:64, :].bitcast(I32), 0)
            nc.vector.memset(rows[64:P, :].bitcast(I32), 0)
            return rows

        def zeroed_planes(tile, engine):
            engine.memset(tile[:].bitcast(I32), 0)
            return tile

        def spread_scale_rows(queue, planes, rows):
            for quad in range(4):
                queue.dma_start(
                    planes[32 * quad : 32 * quad + 4, :, :].bitcast(I32), rows[8 * quad : 8 * quad + 8, :].bitcast(I32)
                )

        def load_table_words(a, slot):
            words = in_slot(slot, [P, T], U16, "table_words%d" % a)
            nc.sync.dma_start(words[:].bitcast(I32), tab_words[a].bitcast(I32))
            return words

        def load_w2_words(b, slot):
            words = in_slot(slot, [P, 2, PASS], I32, "w2_words%d" % b)
            both_passes = w2_words.rearrange("a p c i -> p a (c i)").bitcast(I32)
            nc.sync.dma_start(words[:], both_passes[:, :, PASS * b : PASS * (b + 1)])
            return words

        def load_rows(rows, slot, name):
            raw = in_slot(slot, [P, PACK, rows.shape[1]], F32, name)
            nc.sync.dma_start(raw[:], rows.rearrange("(p j) c -> p j c", j=PACK))
            return raw

        def load_w1(a, b, slot):
            return load_rows(w1[PASS * a : PASS * (a + 1), PASS * b : PASS * (b + 1)], slot, "w1_%d%d" % (a, b))

        def load_w4(b, slot):
            return load_rows(w4[PASS * b : PASS * (b + 1), :], slot, "w4_%d" % b)

        def quantise(woven, name):
            width = woven.shape[1] // PACK
            codes = keep.tile([P, width], U32, name=name + "_codes", align_bytes=64)
            plane = keep.tile([P, width], U8, name=name + "_plane", align_bytes=64)
            nc.vector.quantize_mx(out=codes[:].bitcast(FP8X4), scales=plane[:], in_=woven[:])
            return codes[:], plane[:]

        w1q, w2q, w4q = {}, {}, {}

        def quantise_w1(a, b, raw, copy, slot):
            woven = in_slot(slot, [P, PASS * PACK], BF16, "w1_woven")
            copy(
                woven[:].rearrange("p (t m j) -> p m j t", t=PACK, j=PACK),
                raw[:].rearrange("p j (m t) -> p m j t", t=PACK),
            )
            w1q[(a, b)] = quantise(woven, "w1_%d%d" % (a, b))

        def quantise_w4(b, raw):
            woven = in_slot("w4_woven", [P, N * PACK], BF16, "w4_woven")
            nc.scalar.copy(
                woven[:].rearrange("p (c i j) -> p c j i", i=4, j=PACK),
                raw[:].rearrange("p j (c i) -> p c j i", i=4),
            )
            w4q[b] = quantise(woven, "w4_%d" % b)

        def deal_w2_words(b, raw):
            codes = keep.tile([P, 2, PASS], I32, name="w2_codes%d" % b, align_bytes=64)
            nc.vector.tensor_copy(
                codes[:].rearrange("p a (t c i) -> p a c t i", t=PACK, i=4),
                raw[:].rearrange("p a (c i t) -> p a c t i", t=PACK, i=4),
            )
            for a in range(2):
                w2q[(a, b)] = (codes[:, a, :], w2_planes[:, a, PASS * b : PASS * (b + 1)])

        offs_t = load_list(offs, "offs")
        w2_rows = load_scale_rows(w2_scales, "w2_rows", "w2_rows")
        table_rows = load_scale_rows(tab_scales, "slot_a", "table_rows")
        pos2_t = load_list(pos2, "pos2")
        pos1_t = load_list(pos1, "pos1")
        table0 = load_table_words(0, "slot_b")
        w1_00 = load_w1(0, 0, "slot_c")
        w2_words0 = load_w2_words(0, "slot_h")
        zero = keep.tile([P, 2], F32, name="zero")
        nc.gpsimd.memset(zero[:, 0:1], 0.0)
        nc.scalar.activation(zero[:, 1:2], zero[:, 0:1], ACT.Silu)
        w2_planes = zeroed_planes(keep.tile([P, 2, H], U8, name="w2_planes", align_bytes=64), nc.gpsimd)
        vectors = keep.tile([P, 3, 2, PACK], F32, name="vectors")
        for i, vector in enumerate((b1, gz, gt)):
            nc.gpsimd.dma_start(vectors[:, i, :, :], vector.rearrange("(b p t) -> p b t", b=2, t=PACK))
        bias = vectors[:, 0, :, :]
        gain = {"z": vectors[:, 1, :, :], "x": vectors[:, 2, :, :]}
        table_planes = zeroed_planes(keep.tile([P, 2, S], U8, name="table_planes", align_bytes=64), nc.vector)

        w2_rows_dealt = keep.tile([P, H], U8, name="w2_rows_dealt", align_bytes=64)
        nc.vector.tensor_copy(
            w2_rows_dealt[:].rearrange("p (b t c i) -> p b c t i", b=2, t=PACK, i=16),
            w2_rows[:].rearrange("p (b c i t) -> p b c t i", b=2, t=PACK, i=16),
        )
        spread_scale_rows(nc.scalar, w2_planes, w2_rows_dealt)

        picked_rows = keep.tile([P, S], U8, name="picked_rows", align_bytes=64)
        nc.vector.tensor_copy(picked_rows[:], table_rows[:].indirect(offs_t[:]))
        table1 = load_table_words(1, "slot_a")
        spread_scale_rows(nc.sync, table_planes, picked_rows)
        picked = [keep.tile([P, S], U16, name="picked%d" % a, align_bytes=64) for a in range(2)]
        nc.vector.tensor_copy(picked[0][:], table0[:].indirect(offs_t[:]))
        w1_10 = load_w1(1, 0, "slot_b")
        deal_w2_words(0, w2_words0)
        w2_words1 = load_w2_words(1, "slot_h")
        quantise_w1(0, 0, w1_00, nc.scalar.copy, "slot_d")
        for c0 in range(0, S, BANK):
            entries = offs_t[:, c0 // LIST_ROWS : (c0 + BANK) // LIST_ROWS]
            nc.vector.tensor_copy(picked[1][:, c0 : c0 + BANK], table1[:].indirect(entries))
        w3_codes = in_slot("slot_d", [P, 2, 2 * N], U8, "w3_codes")
        nc.sync.dma_start(w3_codes[:].bitcast(I32), w3_words.rearrange("a p c -> p a c").bitcast(I32))

        grip2 = {}
        grip1 = {}
        unscaled = {}

        def first_stage(weights, s, window, func, slice_bias):
            b, t = divmod(s, PACK)
            cols = slice(P * t, P * (t + 1))
            for c0 in range(0, S, BANK):
                bank = psum.tile([P, BANK], F32, name="bank")
                for a in range(2):
                    codes, plane = weights[(a, b)]
                    nc.tensor.matmul_mx(
                        out=bank[:],
                        lhsT=codes[:, cols].bitcast(FP8X4),
                        lhsT_scale=plane[:, cols],
                        rhs=picked[a][:, c0 : c0 + BANK].bitcast(FP4X4),
                        rhs_scale=table_planes[:, a, c0 : c0 + BANK],
                        start=(a == 0),
                        stop=(a == 1),
                    )
                nc.scalar.activation(window[:, c0 : c0 + BANK], bank[:], func, bias=slice_bias)

        def tile_for(name, shape, bufs, slot):
            if slot is None:
                return work.tile(shape, F32, name=name, bufs=bufs)
            return in_slot(slot, shape, F32, name)

        def make_h2(s, window_slot=None):
            h2 = tile_for("h2", [P, S], H2_TILES, window_slot)
            first_stage(w2q, s, h2, ACT.Silu, zero[:, 1:2])
            return h2

        def pick_h2(s, h2):
            b, t = divmod(s, PACK)
            nc.vector.tensor_copy(grip2[b][:, t, :], h2[:].indirect(pos2_t[:]))

        def h2_slice(s):
            pick_h2(s, make_h2(s))

        def h1_slice(s, window_slot=None, grip_slot=None):
            b, t = divmod(s, PACK)
            h1 = tile_for("h1", [P, S], H1_TILES, window_slot)
            first_stage(w1q, s, h1, ACT.Identity, bias[:, b, t : t + 1])
            charge = work.tile([P, PAIRS], F32, name="charge", bufs=2)
            nc.vector.tensor_copy(charge[:], h1[:].indirect(pos1_t[:]))
            grip1[s] = tile_for("grip1", [P, PAIRS], PACK, grip_slot)
            nc.vector.tensor_copy(grip1[s][:], h1[:].indirect(pos2_t[:]))
            if t == 0:
                unscaled[("z", b)] = work.tile([P, PACK, PAIRS], F32, name="least", bufs=2)
            nc.vector.tensor_tensor(unscaled[("z", b)][:, t, :], charge[:], grip2[b][:, t, :], ALU.min)

        def bound(s):
            b, t = divmod(s, PACK)
            nc.scalar.activation(unscaled[("x", b)][:, t, :], grip1[s][:], ACT.Tanh)

        def scale_slice(rows, kind, s):
            b, t = divmod(s, PACK)
            nc.scalar.activation(rows[:, t, :], unscaled[(kind, b)][:, t, :], ACT.Copy, scale=gain[kind][:, b, t : t + 1])

        def by_fours(rows):
            return rows.rearrange("p t (c i) -> p c t i", i=4)

        def woven_tile(width, slot):
            woven = in_slot(slot, [P, width * PACK], BF16, "woven")
            return woven, woven[:].rearrange("p (c i t) -> p c t i", i=4, t=PACK)

        def weave(rows, slot):
            woven, view = woven_tile(rows.shape[2], slot)
            nc.scalar.copy(view, by_fours(rows))
            return woven

        def scale_and_weave(kind, b, m0, slot):
            woven, view = woven_tile(HALF, slot)
            gains = gain[kind][:, b, :].unsqueeze(1).unsqueeze(3).to_broadcast([P, HALF // 4, PACK, 4])
            nc.vector.tensor_tensor(view, by_fours(unscaled[(kind, b)][:, :, m0 : m0 + HALF]), gains, ALU.mult)
            return woven

        sums = {}

        def add_pass(kind, b, operand, m0, h0, first=False, last=False):
            codes, plane = operand
            step = P if kind == "z" else HALF
            for j in range(N // P):
                if first:
                    sums[(h0, j)] = psum.tile([P, HALF], F32, name="sum", tag="bank")
                cols = slice(P * j, P * (j + 1))
                if kind == "z":
                    lhs = w3_codes[:, b, 2 * P * j : 2 * P * (j + 1)].bitcast(FP4X4)
                    lhs_plane = w3_planes[:, b, cols]
                else:
                    lhs = w4q[b][0][:, cols].bitcast(FP8X4)
                    lhs_plane = w4q[b][1][:, cols]
                for c0 in range(0, HALF, step):
                    moving = slice(h0 - m0 + c0, h0 - m0 + c0 + step)
                    nc.tensor.matmul_mx(
                        out=sums[(h0, j)][:, c0 : c0 + step],
                        lhsT=lhs,
                        lhsT_scale=lhs_plane,
                        rhs=codes[:, moving].bitcast(FP8X4),
                        rhs_scale=plane[:, moving],
                        start=first and c0 == 0,
                        stop=last and c0 + step == HALF,
                    )

        def store(h0, copies):
            for j in range(N // P):
                result = work.tile([P, HALF], F32, name="result", bufs=8)
                copies[j % len(copies)](result[:], sums[(h0, j)][:])
                nc.sync.dma_start(out[P * j : P * (j + 1), h0 : h0 + HALF], result[:])

        h2_first = make_h2(0, "slot_c")
        quantise_w1(1, 0, w1_10, nc.vector.tensor_copy, "slot_e")
        w1_11 = load_w1(1, 1, "slot_b")
        deal_w2_words(1, w2_words1)
        grip2[0] = in_slot("slot_e", [P, PACK, PAIRS], F32, "grip2")
        pick_h2(0, h2_first)
        w1_01 = load_w1(0, 1, "slot_c")
        h2_slice(1)
        h2_slice(2)
        h1_slice(0, window_slot="slot_f")
        w4_0 = load_w4(0, "slot_f")
        h2_slice(3)
        w3_planes = zeroed_planes(in_slot("slot_h", [P, 2, N], U8, "w3_planes"), nc.gpsimd)
        for quad in range(4):
            nc.sync.dma_start(
                w3_planes[32 * quad : 32 * quad + 4, :, :].bitcast(I32),
                w3_scales[:, 4 * quad : 4 * quad + 4, :].rearrange("a r c -> r a c").bitcast(I32),
            )
        h1_slice(1, window_slot="slot_i")
        w4_1 = load_w4(1, "slot_i")
        for s in range(2, PACK):
            h1_slice(s)

        quantise_w1(0, 1, w1_01, nc.scalar.copy, "w1_woven_a")
        quantise_w1(1, 1, w1_11, nc.scalar.copy, "w1_woven_b")
        unscaled[("x", 0)] = in_slot("slot_c", [P, PACK, PAIRS], F32, "bounded")
        grip2[1] = in_slot("grip2_1", [P, PACK, PAIRS], F32, "grip2")
        for t in range(PACK - 1):
            h2_slice(PACK + t)
            bound(t)
        h2_slice(SLICES - 1)
        quantise_w4(0, w4_0)
        bound(PACK - 1)

        h1_slice(PACK)
        h1_slice(PACK + 1)
        x_rows = in_slot("slot_g", [P, PACK, PAIRS], BF16, "x_rows")
        for s in range(PACK):
            scale_slice(x_rows, "x", s)
        x_woven = weave(x_rows[:], "x0_woven")
        h1_slice(PACK + 2)
        quantise_w4(1, w4_1)
        h1_slice(PACK + 3, grip_slot="slot_g")
        x0q = quantise(x_woven, "x0")
        for h0 in (0, HALF):
            add_pass("x", 0, x0q, 0, h0, first=True)
        z_rows = in_slot("slot_b", [P, PACK, PAIRS], BF16, "z_rows")
        for s in range(PACK):
            scale_slice(z_rows, "z", s)
        unscaled[("x", 1)] = in_slot("bounded1", [P, PACK, PAIRS], F32, "bounded")
        for s in range(PACK, SLICES):
            bound(s)
        z0q = quantise(weave(z_rows[:], "z0_woven"), "z0")

        for h0, copies in ((0, [nc.scalar.copy]), (HALF, [nc.scalar.copy, nc.vector.tensor_copy])):
            z_woven = scale_and_weave("z", 1, h0, "slot_g")
            x_woven = scale_and_weave("x", 1, h0, "x1_woven")
            add_pass("z", 0, z0q, 0, h0)
            add_pass("z", 1, quantise(z_woven, "z1_%d" % h0), h0, h0)
            add_pass("x", 1, quantise(x_woven, "x1_%d" % h0), h0, h0, last=True)
            store(h0, copies)
